import numpy as np
import ml_dtypes


def mxq(x, axis, fmt="e4m3"):
    dtype, down = {"e4m3": (ml_dtypes.float8_e4m3fn, 7), "e5m2": (ml_dtypes.float8_e5m2, 14)}[fmt]
    v = np.moveaxis(np.asarray(x, np.float32).astype(ml_dtypes.bfloat16).astype(np.float64), axis, -1)
    blocks = v.reshape(v.shape[:-1] + (-1, 32))
    amax = np.abs(blocks).max(-1, keepdims=True)
    byte = np.maximum(np.where(amax > 0, np.frexp(amax)[1] - 1 + 127, 0) - down, 1)
    scale = np.exp2(byte - 127.0)
    codes = (blocks / scale).astype(np.float32).astype(dtype).astype(np.float64)
    return np.moveaxis((codes * scale).reshape(v.shape), -1, axis)


WIDE = False


def mx_kscale(k):
    if not WIDE:
        return np.ones(k)
    levels = np.array([10, -10, 5, -5, 0])
    if k % 512:
        return np.exp2(np.random.permutation(np.resize(levels, k // 32))).repeat(32)
    a = np.empty((k // 512, 16))
    for p in range(k // 512):
        a[p, :8] = np.random.permutation(np.resize(levels, 8))
        for g in range(8):
            far = levels[np.abs(levels - a[p, g]) >= 10]
            a[p, g + 8] = far[np.random.randint(len(far))]
    return np.exp2(a.ravel()).repeat(32)


def f64(x):
    return np.asarray(x).astype(np.float64)


def striped(idx):
    return np.tile(idx.reshape(-1, 16).T, (8, 1)).astype(np.uint16)


def unstriped(offs):
    return offs[:16].T.reshape(-1).astype(np.int64)


def pack_weight(w):
    k, n = w.shape
    w = f64(np.asarray(w, np.float32).astype(ml_dtypes.bfloat16)).reshape(k // 32, 32, n)
    amax = np.abs(w).max(1)
    byte = np.clip(np.where(amax > 0, np.frexp(amax)[1] - 1 + 127 - 7, 1), 1, 254)
    scaled = (w * np.exp2(127.0 - byte)[:, None, :]).reshape(k, n).astype(np.float32)
    words = np.ascontiguousarray(scaled.reshape(k // 512, 128, 4, n).transpose(0, 1, 3, 2)).astype(ml_dtypes.float8_e4m3fn).view(np.uint8)
    return words, np.ascontiguousarray(byte.astype(np.uint8).reshape(k // 512, 16, n))


def unpack_weight(words, scales):
    g, p, n, _ = words.shape
    vals = np.ascontiguousarray(words).view(ml_dtypes.float8_e4m3fn).astype(np.float64) * np.repeat(np.exp2(scales.astype(np.float64) - 127.0), 8, axis=1)[..., None]
    return vals.transpose(0, 1, 3, 2).reshape(g * 512, n)


def relu(v):
    return np.maximum(v, 0.0)

def planes(y):
    n, m = y.shape
    v = y.astype(np.float32).astype(ml_dtypes.bfloat16).astype(np.float64).reshape(n // 32, 32, m)
    top = np.abs(v).max(1)
    byte = np.clip(np.where(top > 0, np.frexp(top)[1] - 1 + 127 - 7, 1), 1, 254)
    codes = (v * np.exp2(127.0 - byte)[:, None, :]).reshape(n, m).astype(np.float32).astype(ml_dtypes.float8_e4m3fn).view(np.uint8)
    words = codes.reshape(n // 512, 128, 4, m).transpose(0, 1, 3, 2)
    return np.ascontiguousarray(words), np.ascontiguousarray(byte.astype(np.uint8).reshape(n // 512, 16, m))


K, T, N = 512, 512, 512


def setup_inputs():
    n = np.random.standard_normal
    s = mx_kscale(K)[:, None]
    packed_xT = pack_weight(n((K, T)) * s)
    return {
        "x_words": packed_xT[0],
        "x_scales": packed_xT[1],
        "w1": (n((K, N)) / np.sqrt(K) / s).astype(np.float32),
        "pos1": striped(np.random.permutation(T)),
        "pos2": striped(np.random.permutation(T)),
        "pos3": striped(np.random.permutation(T)),
    }


def reference(x_words, x_scales, w1, pos1, pos2, pos3):
    xq = unpack_weight(x_words, x_scales)
    y = relu(mxq(f64(w1), 0, "e4m3").T @ xq)
    n0 = y[:, unstriped(pos1)]
    n1 = y[:, unstriped(pos2)]
    n2 = y[:, unstriped(pos3)]
    out_0 = np.maximum(np.minimum(n0, n1), np.minimum(np.maximum(n0, n1), n2))
    return (out_0,) + planes(out_0)

@@ -1,0 +1,136 @@
+from contextlib import ExitStack
+
+import concourse.mybir as mybir
+
+K, T, N = 512, 512, 512
+FLOPS = 2 * K * T * N
+
+F32 = mybir.dt.float32
+BF16 = mybir.dt.bfloat16
+I32 = mybir.dt.int32
+U32 = mybir.dt.uint32
+U16 = mybir.dt.uint16
+U8 = mybir.dt.uint8
+FP8X4 = mybir.dt.float8_e4m3fn_x4
+MIN = mybir.AluOpType.min
+MAX = mybir.AluOpType.max
+RELU = mybir.ActivationFunctionType.Relu
+
+P = 128
+PACK = 4
+W_CHUNKS = ((0, 256), (256, 128), (384, 128))
+V_CHUNKS = ((0, 256), (256, 128), (384, 128))
+
+
+def tile_picked_wmedian_relu_lo_kernel(
+    tc, x_words, x_scales, w1, pos1, pos2, pos3, out_0, out_1, out_2
+):
+    nc = tc.nc
+    with ExitStack() as ctx:
+        keep = ctx.enter_context(tc.tile_pool(name="keep", bufs=1))
+        psum = ctx.enter_context(tc.psum_pool(name="psum", bufs=1))
+
+        lists = [keep.tile([P, T // 16], U16, name=f"list{d}") for d in range(3)]
+        x_plane = keep.tile([P, T], U8, align_bytes=64, name="x_plane")
+        x_codes = keep.tile([P, T], U32, align_bytes=64, name="x_codes")
+        nc.vector.memset(x_plane[:].bitcast(I32), 0)
+
+        w_rows = w1.rearrange("(p j) c -> p j c", j=PACK)
+        w_raw = []
+        for i, (c0, n) in enumerate(W_CHUNKS):
+            raw = keep.tile([P, PACK, n], F32, name=f"w_raw{i}")
+            nc.sync.dma_start(out=raw[:], in_=w_rows[:, :, c0 : c0 + n])
+            w_raw.append(raw)
+        for q in range(4):
+            nc.sync.dma_start(
+                out=x_plane[32 * q : 32 * q + 4, :].bitcast(I32),
+                in_=x_scales[0][4 * q : 4 * q + 4, :].bitcast(I32),
+            )
+        nc.sync.dma_start(
+            out=x_codes[:].bitcast(I32),
+            in_=x_words[0].rearrange("p n t -> p (n t)").bitcast(I32),
+        )
+        for tile, pos in zip(lists, (pos1, pos2, pos3)):
+            nc.sync.dma_start(tile[:], pos)
+
+        w_grouped = keep.tile([P, PACK, P, PACK], BF16, align_bytes=64, name="w_grouped")
+        for raw, (c0, n) in zip(w_raw, W_CHUNKS):
+            nc.vector.tensor_copy(
+                out=w_grouped[:, :, c0 // PACK : (c0 + n) // PACK, :].rearrange("p t m j -> p m j t"),
+                in_=raw[:].rearrange("p j (m t) -> p m j t", t=PACK),
+            )
+
+        ys = []
+        for t in range(PACK):
+            w_codes = keep.tile([P, P], U32, align_bytes=64, name=f"w_codes{t}")
+            w_plane = keep.tile([P, P], U8, align_bytes=64, name=f"w_plane{t}")
+            nc.vector.quantize_mx(
+                out=w_codes[:].bitcast(FP8X4),
+                scales=w_plane[:],
+                in_=w_grouped[:, t, :, :].rearrange("p m j -> p (m j)"),
+            )
+            y = keep.tile([P, T], F32, name=f"y{t}")
+            halves = 2 if t == 0 else 1
+            width = T // halves
+            for h in range(halves):
+                cols = slice(h * width, (h + 1) * width)
+                acc = psum.tile([P, width], F32, name=f"acc{t}_{h}")
+                nc.tensor.matmul_mx(
+                    out=acc[:],
+                    lhsT=w_codes[:].bitcast(FP8X4),
+                    lhsT_scale=w_plane[:],
+                    rhs=x_codes[:, cols].bitcast(FP8X4),
+                    rhs_scale=x_plane[:, cols],
+                    start=True,
+                    stop=True,
+                )
+                if halves == 2 and h == 0:
+                    nc.vector.tensor_scalar(y[:, cols], acc[:], 0.0, None, MAX)
+                else:
+                    nc.scalar.activation(y[:, cols], acc[:], RELU)
+            ys.append(y)
+
+        out_rows = out_0.rearrange("(p t) v -> p t v", t=PACK)
+        out_words = out_1[0].rearrange("p n t -> p (n t)")
+        o_plane = keep.tile([P, T], U8, align_bytes=64, name="o_plane")
+        for i, (v0, n) in enumerate(V_CHUNKS):
+            last = i == len(V_CHUNKS) - 1
+            offs = slice(v0 // 16, (v0 + n) // 16)
+            a, b, c, lo, hi, mid, med = (
+                keep.tile([P, PACK, n], F32, name=f"{nm}{i}")
+                for nm in ("a", "b", "c", "lo", "hi", "mid", "med")
+            )
+            groups = [slice(t, t + 1) for t in range(PACK)] if last else [slice(0, PACK)]
+            for g in groups:
+                for t in range(g.start, g.stop):
+                    for dst, lst in zip((a, b, c), lists):
+                        nc.vector.tensor_copy(dst[:, t, :], ys[t][:].indirect(lst[:, offs]))
+                nc.vector.tensor_tensor(hi[:, g, :], a[:, g, :], b[:, g, :], MAX)
+                nc.vector.tensor_tensor(lo[:, g, :], a[:, g, :], b[:, g, :], MIN)
+                nc.vector.tensor_tensor(mid[:, g, :], hi[:, g, :], c[:, g, :], MIN)
+                nc.vector.tensor_tensor(med[:, g, :], lo[:, g, :], mid[:, g, :], MAX)
+            nc.sync.dma_start(out=out_rows[:, :, v0 : v0 + n], in_=med[:])
+
+            grouped = keep.tile([P, n, PACK], BF16, align_bytes=64, name=f"grouped{i}")
+            o_codes = keep.tile([P, n], U32, align_bytes=64, name=f"o_codes{i}")
+            dst = grouped[:].rearrange("p (c i) t -> p c t i", i=4)
+            src = med[:].rearrange("p t (c i) -> p c t i", i=4)
+            if last:
+                nc.vector.tensor_copy(out=dst, in_=src)
+            else:
+                nc.scalar.copy(out=dst, in_=src)
+            nc.vector.quantize_mx(
+                out=o_codes[:].bitcast(FP8X4),
+                scales=o_plane[:, v0 : v0 + n],
+                in_=grouped[:].rearrange("p v t -> p (v t)"),
+            )
+            nc.sync.dma_start(
+                out=out_words[:, PACK * v0 : PACK * (v0 + n)].bitcast(I32),
+                in_=o_codes[:].bitcast(I32),
+            )
+        for q in range(4):
+            queue = nc.scalar if q % 2 == 0 else nc.sync
+            queue.dma_start(
+                out=out_2[0][4 * q : 4 * q + 4, :].bitcast(I32),
+                in_=o_plane[32 * q : 32 * q + 4, :].bitcast(I32),
+            )

@@ -1,6 +1,7 @@
 from contextlib import ExitStack
 
 import concourse.mybir as mybir
+from concourse.masks import make_identity
 
 K, T, N = 512, 512, 512
 FLOPS = 2 * K * T * N
@@ -14,12 +15,18 @@ U8 = mybir.dt.uint8
 FP8X4 = mybir.dt.float8_e4m3fn_x4
 MIN = mybir.AluOpType.min
 MAX = mybir.AluOpType.max
+ADD = mybir.AluOpType.add
+SUB = mybir.AluOpType.subtract
+ABS = mybir.ActivationFunctionType.Abs
+COPY = mybir.ActivationFunctionType.Copy
 RELU = mybir.ActivationFunctionType.Relu
 
 P = 128
 PACK = 4
 W_CHUNKS = ((0, 256), (256, 128), (384, 128))
-V_CHUNKS = ((0, 256), (256, 128), (384, 128))
+HALF = T // 2
+PAIR = 2
+BLOCKS = PAIR * HALF // P
 
 
 def tile_picked_wmedian_relu_lo_kernel(
@@ -34,6 +41,9 @@ def tile_picked_wmedian_relu_lo_kernel(
         x_plane = keep.tile([P, T], U8, align_bytes=64, name="x_plane")
         x_codes = keep.tile([P, T], U32, align_bytes=64, name="x_codes")
         nc.vector.memset(x_plane[:].bitcast(I32), 0)
+
+        ident = keep.tile([P, P], F32, name="ident")
+        make_identity(nc, ident[:])
 
         w_rows = w1.rearrange("(p j) c -> p j c", j=PACK)
         w_raw = []
@@ -50,8 +60,8 @@ def tile_picked_wmedian_relu_lo_kernel(
             out=x_codes[:].bitcast(I32),
             in_=x_words[0].rearrange("p n t -> p (n t)").bitcast(I32),
         )
-        for tile, pos in zip(lists, (pos1, pos2, pos3)):
-            nc.sync.dma_start(tile[:], pos)
+        for d, pos in ((1, pos2), (0, pos1), (2, pos3)):
+            nc.sync.dma_start(lists[d][:], pos)
 
         w_grouped = keep.tile([P, PACK, P, PACK], BF16, align_bytes=64, name="w_grouped")
         for raw, (c0, n) in zip(w_raw, W_CHUNKS):
@@ -93,32 +103,78 @@ def tile_picked_wmedian_relu_lo_kernel(
         out_rows = out_0.rearrange("(p t) v -> p t v", t=PACK)
         out_words = out_1[0].rearrange("p n t -> p (n t)")
         o_plane = keep.tile([P, T], U8, align_bytes=64, name="o_plane")
-        for i, (v0, n) in enumerate(V_CHUNKS):
-            last = i == len(V_CHUNKS) - 1
-            offs = slice(v0 // 16, (v0 + n) // 16)
-            a, b, c, lo, hi, mid, med = (
-                keep.tile([P, PACK, n], F32, name=f"{nm}{i}")
-                for nm in ("a", "b", "c", "lo", "hi", "mid", "med")
-            )
-            groups = [slice(t, t + 1) for t in range(PACK)] if last else [slice(0, PACK)]
-            for g in groups:
-                for t in range(g.start, g.stop):
-                    for dst, lst in zip((a, b, c), lists):
-                        nc.vector.tensor_copy(dst[:, t, :], ys[t][:].indirect(lst[:, offs]))
-                nc.vector.tensor_tensor(hi[:, g, :], a[:, g, :], b[:, g, :], MAX)
-                nc.vector.tensor_tensor(lo[:, g, :], a[:, g, :], b[:, g, :], MIN)
-                nc.vector.tensor_tensor(mid[:, g, :], hi[:, g, :], c[:, g, :], MIN)
-                nc.vector.tensor_tensor(med[:, g, :], lo[:, g, :], mid[:, g, :], MAX)
-            nc.sync.dma_start(out=out_rows[:, :, v0 : v0 + n], in_=med[:])
+        units = [(h, g) for h in range(2) for g in range(2)]
+        med = [keep.tile([P, PACK, HALF], F32, name=f"med{h}") for h in range(2)]
 
-            grouped = keep.tile([P, n, PACK], BF16, align_bytes=64, name=f"grouped{i}")
-            o_codes = keep.tile([P, n], U32, align_bytes=64, name=f"o_codes{i}")
-            dst = grouped[:].rearrange("p (c i) t -> p c t i", i=4)
-            src = med[:].rearrange("p t (c i) -> p c t i", i=4)
-            if last:
-                nc.vector.tensor_copy(out=dst, in_=src)
-            else:
-                nc.scalar.copy(out=dst, in_=src)
+        def unit_tile(name):
+            return keep.tile([P, PAIR, HALF], F32, name=name)
+
+        def flat(tile):
+            return tile[:].rearrange("p t v -> p (t v)")
+
+        def window(u, t, d):
+            h, g = units[u]
+            return ys[PAIR * g + t][:].indirect(lists[d][:, h * HALF // 16 : (h + 1) * HALF // 16])
+
+        def turned_sum(terms, tag):
+            bank = psum.tile([P, PAIR * HALF], F32, name=tag)
+            for k in range(BLOCKS):
+                cols = slice(k * P, (k + 1) * P)
+                for i, term in enumerate(terms):
+                    nc.tensor.matmul(
+                        bank[:, cols], term[:, cols], ident[:],
+                        start=(i == 0), stop=(i == len(terms) - 1), is_transpose=True,
+                    )
+            return bank
+
+        a, b, lo, e, f, width_of = {}, {}, {}, {}, {}, {}
+
+        def fetch_pair(u):
+            a[u] = e[u - 2] if u >= 2 else unit_tile(f"a{u}")
+            b[u] = lo[u - 2] if u >= 2 else unit_tile(f"b{u}")
+            minus_b = unit_tile("minus_b")
+            for t in range(PAIR):
+                nc.vector.tensor_copy(b[u][:, t, :], window(u, t, 1))
+                nc.scalar.activation(minus_b[:, t, :], b[u][:, t, :], COPY, scale=-1.0)
+                nc.vector.tensor_copy(a[u][:, t, :], window(u, t, 0))
+            diff = turned_sum([flat(minus_b), flat(a[u])], "diff")
+            width_turned = unit_tile(f"width_turned{u}")
+            nc.scalar.activation(flat(width_turned), diff[:], ABS)
+            width_of[u] = turned_sum([flat(width_turned)], f"width{u % 2}")
+
+        def finish_unit(u):
+            h, g = units[u]
+            lo[u] = f[u - 1] if u >= 1 else unit_tile(f"lo{u}")
+            e[u] = unit_tile(f"e{u}")
+            f[u] = unit_tile(f"f{u}")
+            dst = med[h][:, PAIR * g : PAIR * (g + 1), :]
+            w_view = width_of[u][:].rearrange("p (t v) -> p t v", t=PAIR)
+            for t in range(PAIR):
+                nc.vector.tensor_tensor(lo[u][:, t, :], a[u][:, t, :], b[u][:, t, :], MIN)
+            for t in range(PAIR):
+                nc.vector.tensor_tensor(e[u][:, t, :], window(u, t, 2), lo[u][:, t, :], SUB)
+            n = HALF // 2
+            pieces = [slice(i * n, (i + 1) * n) for i in range(2)]
+            for cols in pieces:
+                nc.vector.scalar_tensor_tensor(
+                    f[u][:, :, cols], e[u][:, :, cols], 0.0, w_view[:, :, cols], MAX, MIN
+                )
+            for cols in pieces:
+                nc.vector.tensor_tensor(dst[:, :, cols], f[u][:, :, cols], lo[u][:, :, cols], ADD)
+            for cols in pieces if u == len(units) - 1 else [slice(0, HALF)]:
+                nc.sync.dma_start(
+                    out=out_rows[:, PAIR * g : PAIR * (g + 1), h * HALF + cols.start : h * HALF + cols.stop],
+                    in_=dst[:, :, cols],
+                )
+
+        def planes(v0, n, copy):
+            h, c0 = divmod(v0, HALF)
+            grouped = keep.tile([P, n, PACK], BF16, align_bytes=64, name=f"grouped{v0}")
+            o_codes = keep.tile([P, n], U32, align_bytes=64, name=f"o_codes{v0}")
+            copy(
+                out=grouped[:].rearrange("p (c i) t -> p c t i", i=4),
+                in_=med[h][:, :, c0 : c0 + n].rearrange("p t (c i) -> p c t i", i=4),
+            )
             nc.vector.quantize_mx(
                 out=o_codes[:].bitcast(FP8X4),
                 scales=o_plane[:, v0 : v0 + n],
@@ -128,6 +184,18 @@ def tile_picked_wmedian_relu_lo_kernel(
                 out=out_words[:, PACK * v0 : PACK * (v0 + n)].bitcast(I32),
                 in_=o_codes[:].bitcast(I32),
             )
+
+        fetch_pair(0)
+        fetch_pair(1)
+        finish_unit(0)
+        fetch_pair(2)
+        finish_unit(1)
+        fetch_pair(3)
+        finish_unit(2)
+        planes(0, HALF, nc.scalar.copy)
+        finish_unit(3)
+        planes(HALF, HALF // 2, nc.scalar.copy)
+        planes(HALF + HALF // 2, HALF // 2, nc.vector.tensor_copy)
         for q in range(4):
             queue = nc.scalar if q % 2 == 0 else nc.sync
             queue.dma_start(

@@ -65,10 +65,11 @@ def tile_picked_wmedian_relu_lo_kernel(
 
         w_grouped = keep.tile([P, PACK, P, PACK], BF16, align_bytes=64, name="w_grouped")
         for raw, (c0, n) in zip(w_raw, W_CHUNKS):
-            nc.vector.tensor_copy(
-                out=w_grouped[:, :, c0 // PACK : (c0 + n) // PACK, :].rearrange("p t m j -> p m j t"),
-                in_=raw[:].rearrange("p j (m t) -> p m j t", t=PACK),
-            )
+            dealt = w_grouped[:, :, c0 // PACK : (c0 + n) // PACK, :].rearrange("p t m j -> p m j t")
+            source = raw[:].rearrange("p j (m t) -> p m j t", t=PACK)
+            parts = (slice(0, 1), slice(1, PACK)) if c0 + n == N else (slice(0, PACK),)
+            for ts in parts:
+                nc.vector.tensor_copy(out=dealt[:, :, :, ts], in_=source[:, :, :, ts])
 
         ys = []
         for t in range(PACK):
@@ -94,10 +95,7 @@ def tile_picked_wmedian_relu_lo_kernel(
                     start=True,
                     stop=True,
                 )
-                if halves == 2 and h == 0:
-                    nc.vector.tensor_scalar(y[:, cols], acc[:], 0.0, None, MAX)
-                else:
-                    nc.scalar.activation(y[:, cols], acc[:], RELU)
+                nc.scalar.activation(y[:, cols], acc[:], RELU)
             ys.append(y)
 
         out_rows = out_0.rearrange("(p t) v -> p t v", t=PACK)
@@ -142,6 +140,9 @@ def tile_picked_wmedian_relu_lo_kernel(
             nc.scalar.activation(flat(width_turned), diff[:], ABS)
             width_of[u] = turned_sum([flat(width_turned)], f"width{u % 2}")
 
+        def runs(ap):
+            return ap.rearrange("p (r v) -> p r v", r=PAIR)
+
         def finish_unit(u):
             h, g = units[u]
             lo[u] = f[u - 1] if u >= 1 else unit_tile(f"lo{u}")
@@ -155,12 +156,22 @@ def tile_picked_wmedian_relu_lo_kernel(
                 nc.vector.tensor_tensor(e[u][:, t, :], window(u, t, 2), lo[u][:, t, :], SUB)
             n = HALF // 2
             pieces = [slice(i * n, (i + 1) * n) for i in range(2)]
-            for cols in pieces:
-                nc.vector.scalar_tensor_tensor(
-                    f[u][:, :, cols], e[u][:, :, cols], 0.0, w_view[:, :, cols], MAX, MIN
-                )
-            for cols in pieces:
-                nc.vector.tensor_tensor(dst[:, :, cols], f[u][:, :, cols], lo[u][:, :, cols], ADD)
+            if u < 2:
+                for t in range(PAIR):
+                    nc.vector.scalar_tensor_tensor(
+                        f[u][:, :, pieces[t]], runs(e[u][:, t, :]), 0.0, runs(w_view[:, t, :]), MAX, MIN
+                    )
+                for t in range(PAIR):
+                    nc.gpsimd.tensor_tensor(
+                        runs(dst[:, t, :]), f[u][:, :, pieces[t]], runs(lo[u][:, t, :]), ADD
+                    )
+            else:
+                for cols in pieces:
+                    nc.vector.scalar_tensor_tensor(
+                        f[u][:, :, cols], e[u][:, :, cols], 0.0, w_view[:, :, cols], MAX, MIN
+                    )
+                for cols in pieces:
+                    nc.vector.tensor_tensor(dst[:, :, cols], f[u][:, :, cols], lo[u][:, :, cols], ADD)
             for cols in pieces if u == len(units) - 1 else [slice(0, HALF)]:
                 nc.sync.dma_start(
                     out=out_rows[:, PAIR * g : PAIR * (g + 1), h * HALF + cols.start : h * HALF + cols.stop],

@@ -125,50 +125,47 @@ def tile_picked_wmedian_relu_lo_kernel(
                     )
             return bank
 
-        a, b, lo, e, f, width_of = {}, {}, {}, {}, {}, {}
+        lo, f, pairs, width_of = {}, {}, {}, {}
+        quarter = HALF // 2
+        pieces = [slice(i * quarter, (i + 1) * quarter) for i in range(2)]
 
         def fetch_pair(u):
-            a[u] = e[u - 2] if u >= 2 else unit_tile(f"a{u}")
-            b[u] = lo[u - 2] if u >= 2 else unit_tile(f"b{u}")
+            if u not in pairs:
+                pairs[u] = keep.tile([P, 2, PAIR, HALF], F32, name=f"pairs{u}")
+            a, b = pairs[u][:, 0], pairs[u][:, 1]
             minus_b = unit_tile("minus_b")
             for t in range(PAIR):
-                nc.vector.tensor_copy(b[u][:, t, :], window(u, t, 1))
-                nc.scalar.activation(minus_b[:, t, :], b[u][:, t, :], COPY, scale=-1.0)
-                nc.vector.tensor_copy(a[u][:, t, :], window(u, t, 0))
-            diff = turned_sum([flat(minus_b), flat(a[u])], "diff")
+                nc.vector.tensor_copy(b[:, t, :], window(u, t, 1))
+                nc.scalar.activation(minus_b[:, t, :], b[:, t, :], COPY, scale=-1.0)
+                nc.vector.tensor_copy(a[:, t, :], window(u, t, 0))
+            diff = turned_sum([flat(minus_b), a.rearrange("p t v -> p (t v)")], "diff")
             width_turned = unit_tile(f"width_turned{u}")
             nc.scalar.activation(flat(width_turned), diff[:], ABS)
             width_of[u] = turned_sum([flat(width_turned)], f"width{u % 2}")
 
-        def runs(ap):
-            return ap.rearrange("p (r v) -> p r v", r=PAIR)
-
         def finish_unit(u):
             h, g = units[u]
+            a, b = pairs[u][:, 0], pairs[u][:, 1]
             lo[u] = f[u - 1] if u >= 1 else unit_tile(f"lo{u}")
-            e[u] = unit_tile(f"e{u}")
             f[u] = unit_tile(f"f{u}")
+            pairs[u + 2] = keep.tile([P, 2, PAIR, HALF], F32, name=f"pairs{u + 2}")
+            e = pairs[u + 2][:].rearrange("p s t v -> p s (t v)")[:, :, quarter : quarter + HALF]
             dst = med[h][:, PAIR * g : PAIR * (g + 1), :]
             w_view = width_of[u][:].rearrange("p (t v) -> p t v", t=PAIR)
             for t in range(PAIR):
-                nc.vector.tensor_tensor(lo[u][:, t, :], a[u][:, t, :], b[u][:, t, :], MIN)
+                nc.vector.tensor_tensor(lo[u][:, t, :], a[:, t, :], b[:, t, :], MIN)
             for t in range(PAIR):
-                nc.vector.tensor_tensor(e[u][:, t, :], window(u, t, 2), lo[u][:, t, :], SUB)
-            n = HALF // 2
-            pieces = [slice(i * n, (i + 1) * n) for i in range(2)]
+                nc.vector.tensor_tensor(e[:, t, :], window(u, t, 2), lo[u][:, t, :], SUB)
             if u < 2:
                 for t in range(PAIR):
                     nc.vector.scalar_tensor_tensor(
-                        f[u][:, :, pieces[t]], runs(e[u][:, t, :]), 0.0, runs(w_view[:, t, :]), MAX, MIN
+                        f[u][:, t, :], e[:, t, :], 0.0, w_view[:, t, :], MAX, MIN
                     )
-                for t in range(PAIR):
-                    nc.gpsimd.tensor_tensor(
-                        runs(dst[:, t, :]), f[u][:, :, pieces[t]], runs(lo[u][:, t, :]), ADD
-                    )
+                nc.gpsimd.tensor_tensor(dst.rearrange("p t v -> p (t v)"), flat(f[u]), flat(lo[u]), ADD)
             else:
                 for cols in pieces:
                     nc.vector.scalar_tensor_tensor(
-                        f[u][:, :, cols], e[u][:, :, cols], 0.0, w_view[:, :, cols], MAX, MIN
+                        f[u][:, :, cols], e[:, :, cols], 0.0, w_view[:, :, cols], MAX, MIN
                     )
                 for cols in pieces:
                     nc.vector.tensor_tensor(dst[:, :, cols], f[u][:, :, cols], lo[u][:, :, cols], ADD)

@@ -23,10 +23,16 @@ RELU = mybir.ActivationFunctionType.Relu
 
 P = 128
 PACK = 4
-W_CHUNKS = ((0, 256), (256, 128), (384, 128))
+QUADRANTS = 4
+PER_COLUMN = 16
+LINE = 4
+W_PIECES = ((0, 256), (256, 128), (384, 128))
 HALF = T // 2
+QUARTER = HALF // 2
+EIGHTH = QUARTER // 2
 PAIR = 2
-BLOCKS = PAIR * HALF // P
+UNITS = tuple((h, g) for h in range(T // HALF) for g in range(PACK // PAIR))
+AHEAD = 2
 
 
 def tile_picked_wmedian_relu_lo_kernel(
@@ -37,7 +43,7 @@ def tile_picked_wmedian_relu_lo_kernel(
         keep = ctx.enter_context(tc.tile_pool(name="keep", bufs=1))
         psum = ctx.enter_context(tc.psum_pool(name="psum", bufs=1))
 
-        lists = [keep.tile([P, T // 16], U16, name=f"list{d}") for d in range(3)]
+        lists = [keep.tile([P, T // PER_COLUMN], U16, name=f"list{d}") for d in range(3)]
         x_plane = keep.tile([P, T], U8, align_bytes=64, name="x_plane")
         x_codes = keep.tile([P, T], U32, align_bytes=64, name="x_codes")
         nc.vector.memset(x_plane[:].bitcast(I32), 0)
@@ -47,11 +53,11 @@ def tile_picked_wmedian_relu_lo_kernel(
 
         w_rows = w1.rearrange("(p j) c -> p j c", j=PACK)
         w_raw = []
-        for i, (c0, n) in enumerate(W_CHUNKS):
+        for i, (c0, n) in enumerate(W_PIECES):
             raw = keep.tile([P, PACK, n], F32, name=f"w_raw{i}")
             nc.sync.dma_start(out=raw[:], in_=w_rows[:, :, c0 : c0 + n])
             w_raw.append(raw)
-        for q in range(4):
+        for q in range(QUADRANTS):
             nc.sync.dma_start(
                 out=x_plane[32 * q : 32 * q + 4, :].bitcast(I32),
                 in_=x_scales[0][4 * q : 4 * q + 4, :].bitcast(I32),
@@ -64,12 +70,12 @@ def tile_picked_wmedian_relu_lo_kernel(
             nc.sync.dma_start(lists[d][:], pos)
 
         w_grouped = keep.tile([P, PACK, P, PACK], BF16, align_bytes=64, name="w_grouped")
-        for raw, (c0, n) in zip(w_raw, W_CHUNKS):
-            dealt = w_grouped[:, :, c0 // PACK : (c0 + n) // PACK, :].rearrange("p t m j -> p m j t")
-            source = raw[:].rearrange("p j (m t) -> p m j t", t=PACK)
+        for raw, (c0, n) in zip(w_raw, W_PIECES):
+            dealt = w_grouped[:, :, c0 // PACK : (c0 + n) // PACK, :].rearrange("p t i j -> p i j t")
+            source = raw[:].rearrange("p j (i t) -> p i j t", t=PACK)
             parts = (slice(0, 1), slice(1, PACK)) if c0 + n == N else (slice(0, PACK),)
-            for ts in parts:
-                nc.vector.tensor_copy(out=dealt[:, :, :, ts], in_=source[:, :, :, ts])
+            for slots in parts:
+                nc.vector.tensor_copy(out=dealt[:, :, :, slots], in_=source[:, :, :, slots])
 
         ys = []
         for t in range(PACK):
@@ -78,14 +84,14 @@ def tile_picked_wmedian_relu_lo_kernel(
             nc.vector.quantize_mx(
                 out=w_codes[:].bitcast(FP8X4),
                 scales=w_plane[:],
-                in_=w_grouped[:, t, :, :].rearrange("p m j -> p (m j)"),
+                in_=w_grouped[:, t, :, :].rearrange("p i j -> p (i j)"),
             )
             y = keep.tile([P, T], F32, name=f"y{t}")
-            halves = 2 if t == 0 else 1
-            width = T // halves
-            for h in range(halves):
-                cols = slice(h * width, (h + 1) * width)
-                acc = psum.tile([P, width], F32, name=f"acc{t}_{h}")
+            passes = 2 if t == 0 else 1
+            nodes = T // passes
+            for s in range(passes):
+                cols = slice(s * nodes, (s + 1) * nodes)
+                acc = psum.tile([P, nodes], F32, name=f"acc{t}_{s}")
                 nc.tensor.matmul_mx(
                     out=acc[:],
                     lhsT=w_codes[:].bitcast(FP8X4),
@@ -101,110 +107,123 @@ def tile_picked_wmedian_relu_lo_kernel(
         out_rows = out_0.rearrange("(p t) v -> p t v", t=PACK)
         out_words = out_1[0].rearrange("p n t -> p (n t)")
         o_plane = keep.tile([P, T], U8, align_bytes=64, name="o_plane")
-        units = [(h, g) for h in range(2) for g in range(2)]
-        med = [keep.tile([P, PACK, HALF], F32, name=f"med{h}") for h in range(2)]
+        median = [keep.tile([P, PACK, HALF], F32, name=f"med{h}") for h in range(T // HALF)]
 
         def unit_tile(name):
             return keep.tile([P, PAIR, HALF], F32, name=name)
 
-        def flat(tile):
-            return tile[:].rearrange("p t v -> p (t v)")
+        def flat(ap):
+            return ap.rearrange("p t v -> p (t v)")
 
-        def window(u, t, d):
-            h, g = units[u]
-            return ys[PAIR * g + t][:].indirect(lists[d][:, h * HALF // 16 : (h + 1) * HALF // 16])
+        def looked_up(u, t, d):
+            h, g = UNITS[u]
+            entries = slice(h * HALF // PER_COLUMN, (h + 1) * HALF // PER_COLUMN)
+            return ys[PAIR * g + t][:].indirect(lists[d][:, entries])
 
         def turned_sum(terms, tag):
             bank = psum.tile([P, PAIR * HALF], F32, name=tag)
-            for k in range(BLOCKS):
-                cols = slice(k * P, (k + 1) * P)
+            for c0 in range(0, PAIR * HALF, P):
+                cols = slice(c0, c0 + P)
                 for i, term in enumerate(terms):
                     nc.tensor.matmul(
-                        bank[:, cols], term[:, cols], ident[:],
-                        start=(i == 0), stop=(i == len(terms) - 1), is_transpose=True,
+                        bank[:, cols],
+                        term[:, cols],
+                        ident[:],
+                        start=(i == 0),
+                        stop=(i == len(terms) - 1),
+                        is_transpose=True,
                     )
             return bank
 
-        lo, f, pairs, width_of = {}, {}, {}, {}
-        quarter = HALF // 2
-        pieces = [slice(i * quarter, (i + 1) * quarter) for i in range(2)]
+        def pair_tile(u):
+            return keep.tile([P, 2, PAIR, HALF], F32, name=f"pairs{u}")
+
+        lo, clamped, pairs, width = {}, {}, {}, {}
+        quarters = [slice(0, QUARTER), slice(QUARTER, HALF)]
+        last_pieces = [slice(0, QUARTER), slice(QUARTER, QUARTER + EIGHTH), slice(QUARTER + EIGHTH, HALF)]
 
         def fetch_pair(u):
-            if u not in pairs:
-                pairs[u] = keep.tile([P, 2, PAIR, HALF], F32, name=f"pairs{u}")
+            if u < AHEAD:
+                pairs[u] = pair_tile(u)
             a, b = pairs[u][:, 0], pairs[u][:, 1]
             minus_b = unit_tile("minus_b")
             for t in range(PAIR):
-                nc.vector.tensor_copy(b[:, t, :], window(u, t, 1))
+                nc.vector.tensor_copy(b[:, t, :], looked_up(u, t, 1))
                 nc.scalar.activation(minus_b[:, t, :], b[:, t, :], COPY, scale=-1.0)
-                nc.vector.tensor_copy(a[:, t, :], window(u, t, 0))
-            diff = turned_sum([flat(minus_b), a.rearrange("p t v -> p (t v)")], "diff")
+                nc.vector.tensor_copy(a[:, t, :], looked_up(u, t, 0))
+            diff = turned_sum([flat(minus_b[:]), flat(a)], "diff")
             width_turned = unit_tile(f"width_turned{u}")
-            nc.scalar.activation(flat(width_turned), diff[:], ABS)
-            width_of[u] = turned_sum([flat(width_turned)], f"width{u % 2}")
+            nc.scalar.activation(flat(width_turned[:]), diff[:], ABS)
+            width[u] = turned_sum([flat(width_turned[:])], f"width{u % AHEAD}")
 
         def finish_unit(u):
-            h, g = units[u]
+            h, g = UNITS[u]
+            last = u == len(UNITS) - 1
             a, b = pairs[u][:, 0], pairs[u][:, 1]
-            lo[u] = f[u - 1] if u >= 1 else unit_tile(f"lo{u}")
-            f[u] = unit_tile(f"f{u}")
-            pairs[u + 2] = keep.tile([P, 2, PAIR, HALF], F32, name=f"pairs{u + 2}")
-            e = pairs[u + 2][:].rearrange("p s t v -> p s (t v)")[:, :, quarter : quarter + HALF]
-            dst = med[h][:, PAIR * g : PAIR * (g + 1), :]
-            w_view = width_of[u][:].rearrange("p (t v) -> p t v", t=PAIR)
+            lo[u] = clamped[u - 1] if u > 0 else unit_tile("lo0")
+            clamped[u] = unit_tile(f"clamped{u}")
+            pairs[u + AHEAD] = pair_tile(u + AHEAD)
+            above = pairs[u + AHEAD][:].rearrange("p s t v -> p s (t v)")[:, :, QUARTER : QUARTER + HALF]
+            result = median[h][:, PAIR * g : PAIR * (g + 1), :]
+            bound = width[u][:].rearrange("p (t v) -> p t v", t=PAIR)
             for t in range(PAIR):
                 nc.vector.tensor_tensor(lo[u][:, t, :], a[:, t, :], b[:, t, :], MIN)
             for t in range(PAIR):
-                nc.vector.tensor_tensor(e[:, t, :], window(u, t, 2), lo[u][:, t, :], SUB)
-            if u < 2:
+                nc.vector.tensor_tensor(above[:, t, :], looked_up(u, t, 2), lo[u][:, t, :], SUB)
+            if u + AHEAD < len(UNITS):
                 for t in range(PAIR):
                     nc.vector.scalar_tensor_tensor(
-                        f[u][:, t, :], e[:, t, :], 0.0, w_view[:, t, :], MAX, MIN
+                        clamped[u][:, t, :], above[:, t, :], 0.0, bound[:, t, :], MAX, MIN
                     )
-                nc.gpsimd.tensor_tensor(dst.rearrange("p t v -> p (t v)"), flat(f[u]), flat(lo[u]), ADD)
+                nc.gpsimd.tensor_tensor(flat(result), flat(clamped[u][:]), flat(lo[u][:]), ADD)
             else:
-                for cols in pieces:
+                for cols in quarters:
                     nc.vector.scalar_tensor_tensor(
-                        f[u][:, :, cols], e[:, :, cols], 0.0, w_view[:, :, cols], MAX, MIN
+                        clamped[u][:, :, cols], above[:, :, cols], 0.0, bound[:, :, cols], MAX, MIN
                     )
-                for cols in pieces:
-                    nc.vector.tensor_tensor(dst[:, :, cols], f[u][:, :, cols], lo[u][:, :, cols], ADD)
-            for cols in pieces if u == len(units) - 1 else [slice(0, HALF)]:
+                for cols in last_pieces if last else quarters:
+                    nc.vector.tensor_tensor(
+                        result[:, :, cols], clamped[u][:, :, cols], lo[u][:, :, cols], ADD
+                    )
+            for cols in quarters if last else [slice(0, HALF)]:
+                targets = slice(h * HALF + cols.start, h * HALF + cols.stop)
                 nc.sync.dma_start(
-                    out=out_rows[:, PAIR * g : PAIR * (g + 1), h * HALF + cols.start : h * HALF + cols.stop],
-                    in_=dst[:, :, cols],
+                    out=out_rows[:, PAIR * g : PAIR * (g + 1), targets], in_=result[:, :, cols]
                 )
 
-        def planes(v0, n, copy):
+        def store_codes(v0, n, calls, round_copy):
             h, c0 = divmod(v0, HALF)
             grouped = keep.tile([P, n, PACK], BF16, align_bytes=64, name=f"grouped{v0}")
             o_codes = keep.tile([P, n], U32, align_bytes=64, name=f"o_codes{v0}")
-            copy(
-                out=grouped[:].rearrange("p (c i) t -> p c t i", i=4),
-                in_=med[h][:, :, c0 : c0 + n].rearrange("p t (c i) -> p c t i", i=4),
-            )
-            nc.vector.quantize_mx(
-                out=o_codes[:].bitcast(FP8X4),
-                scales=o_plane[:, v0 : v0 + n],
-                in_=grouped[:].rearrange("p v t -> p (v t)"),
-            )
+            starts = range(0, n, n // calls)
+            for s in starts:
+                round_copy(
+                    out=grouped[:, s : s + n // calls, :].rearrange("p (c i) t -> p c t i", i=LINE),
+                    in_=median[h][:, :, c0 + s : c0 + s + n // calls].rearrange("p t (c i) -> p c t i", i=LINE),
+                )
+            for s in starts:
+                nc.vector.quantize_mx(
+                    out=o_codes[:, s : s + n // calls].bitcast(FP8X4),
+                    scales=o_plane[:, v0 + s : v0 + s + n // calls],
+                    in_=grouped[:, s : s + n // calls, :].rearrange("p v t -> p (v t)"),
+                )
             nc.sync.dma_start(
                 out=out_words[:, PACK * v0 : PACK * (v0 + n)].bitcast(I32),
                 in_=o_codes[:].bitcast(I32),
             )
 
-        fetch_pair(0)
-        fetch_pair(1)
-        finish_unit(0)
-        fetch_pair(2)
-        finish_unit(1)
-        fetch_pair(3)
-        finish_unit(2)
-        planes(0, HALF, nc.scalar.copy)
-        finish_unit(3)
-        planes(HALF, HALF // 2, nc.scalar.copy)
-        planes(HALF + HALF // 2, HALF // 2, nc.vector.tensor_copy)
-        for q in range(4):
+        for u in range(AHEAD):
+            fetch_pair(u)
+        for u in range(len(UNITS) - 1):
+            finish_unit(u)
+            if u + AHEAD < len(UNITS):
+                fetch_pair(u + AHEAD)
+        store_codes(0, HALF, 1, nc.scalar.copy)
+        finish_unit(len(UNITS) - 1)
+        store_codes(HALF, QUARTER, 1, nc.scalar.copy)
+        store_codes(HALF + QUARTER, QUARTER, 2, nc.vector.tensor_copy)
+
+        for q in range(QUADRANTS):
             queue = nc.scalar if q % 2 == 0 else nc.sync
             queue.dma_start(
                 out=out_2[0][4 * q : 4 * q + 4, :].bitcast(I32),

from contextlib import ExitStack

import concourse.mybir as mybir
from concourse.masks import make_identity

K, T, N = 512, 512, 512
FLOPS = 2 * K * T * N

F32 = mybir.dt.float32
BF16 = mybir.dt.bfloat16
I32 = mybir.dt.int32
U32 = mybir.dt.uint32
U16 = mybir.dt.uint16
U8 = mybir.dt.uint8
FP8X4 = mybir.dt.float8_e4m3fn_x4
MIN = mybir.AluOpType.min
MAX = mybir.AluOpType.max
ADD = mybir.AluOpType.add
SUB = mybir.AluOpType.subtract
ABS = mybir.ActivationFunctionType.Abs
COPY = mybir.ActivationFunctionType.Copy
RELU = mybir.ActivationFunctionType.Relu

P = 128
PACK = 4
QUADRANTS = 4
PER_COLUMN = 16
LINE = 4
W_PIECES = ((0, 256), (256, 128), (384, 128))
HALF = T // 2
QUARTER = HALF // 2
EIGHTH = QUARTER // 2
PAIR = 2
UNITS = tuple((h, g) for h in range(T // HALF) for g in range(PACK // PAIR))
AHEAD = 2


def tile_picked_wmedian_relu_lo_kernel(
    tc, x_words, x_scales, w1, pos1, pos2, pos3, out_0, out_1, out_2
):
    nc = tc.nc
    with ExitStack() as ctx:
        keep = ctx.enter_context(tc.tile_pool(name="keep", bufs=1))
        psum = ctx.enter_context(tc.psum_pool(name="psum", bufs=1))

        lists = [keep.tile([P, T // PER_COLUMN], U16, name=f"list{d}") for d in range(3)]
        x_plane = keep.tile([P, T], U8, align_bytes=64, name="x_plane")
        x_codes = keep.tile([P, T], U32, align_bytes=64, name="x_codes")
        nc.vector.memset(x_plane[:].bitcast(I32), 0)

        ident = keep.tile([P, P], F32, name="ident")
        make_identity(nc, ident[:])

        w_rows = w1.rearrange("(p j) c -> p j c", j=PACK)
        w_raw = []
        for i, (c0, n) in enumerate(W_PIECES):
            raw = keep.tile([P, PACK, n], F32, name=f"w_raw{i}")
            nc.sync.dma_start(out=raw[:], in_=w_rows[:, :, c0 : c0 + n])
            w_raw.append(raw)
        for q in range(QUADRANTS):
            nc.sync.dma_start(
                out=x_plane[32 * q : 32 * q + 4, :].bitcast(I32),
                in_=x_scales[0][4 * q : 4 * q + 4, :].bitcast(I32),
            )
        nc.sync.dma_start(
            out=x_codes[:].bitcast(I32),
            in_=x_words[0].rearrange("p n t -> p (n t)").bitcast(I32),
        )
        for d, pos in ((1, pos2), (0, pos1), (2, pos3)):
            nc.sync.dma_start(lists[d][:], pos)

        w_grouped = keep.tile([P, PACK, P, PACK], BF16, align_bytes=64, name="w_grouped")
        for raw, (c0, n) in zip(w_raw, W_PIECES):
            dealt = w_grouped[:, :, c0 // PACK : (c0 + n) // PACK, :].rearrange("p t i j -> p i j t")
            source = raw[:].rearrange("p j (i t) -> p i j t", t=PACK)
            parts = (slice(0, 1), slice(1, PACK)) if c0 + n == N else (slice(0, PACK),)
            for slots in parts:
                nc.vector.tensor_copy(out=dealt[:, :, :, slots], in_=source[:, :, :, slots])

        ys = []
        for t in range(PACK):
            w_codes = keep.tile([P, P], U32, align_bytes=64, name=f"w_codes{t}")
            w_plane = keep.tile([P, P], U8, align_bytes=64, name=f"w_plane{t}")
            nc.vector.quantize_mx(
                out=w_codes[:].bitcast(FP8X4),
                scales=w_plane[:],
                in_=w_grouped[:, t, :, :].rearrange("p i j -> p (i j)"),
            )
            y = keep.tile([P, T], F32, name=f"y{t}")
            passes = 2 if t == 0 else 1
            nodes = T // passes
            for s in range(passes):
                cols = slice(s * nodes, (s + 1) * nodes)
                acc = psum.tile([P, nodes], F32, name=f"acc{t}_{s}")
                nc.tensor.matmul_mx(
                    out=acc[:],
                    lhsT=w_codes[:].bitcast(FP8X4),
                    lhsT_scale=w_plane[:],
                    rhs=x_codes[:, cols].bitcast(FP8X4),
                    rhs_scale=x_plane[:, cols],
                    start=True,
                    stop=True,
                )
                nc.scalar.activation(y[:, cols], acc[:], RELU)
            ys.append(y)

        out_rows = out_0.rearrange("(p t) v -> p t v", t=PACK)
        out_words = out_1[0].rearrange("p n t -> p (n t)")
        o_plane = keep.tile([P, T], U8, align_bytes=64, name="o_plane")
        median = [keep.tile([P, PACK, HALF], F32, name=f"med{h}") for h in range(T // HALF)]

        def unit_tile(name):
            return keep.tile([P, PAIR, HALF], F32, name=name)

        def flat(ap):
            return ap.rearrange("p t v -> p (t v)")

        def looked_up(u, t, d):
            h, g = UNITS[u]
            entries = slice(h * HALF // PER_COLUMN, (h + 1) * HALF // PER_COLUMN)
            return ys[PAIR * g + t][:].indirect(lists[d][:, entries])

        def turned_sum(terms, tag):
            bank = psum.tile([P, PAIR * HALF], F32, name=tag)
            for c0 in range(0, PAIR * HALF, P):
                cols = slice(c0, c0 + P)
                for i, term in enumerate(terms):
                    nc.tensor.matmul(
                        bank[:, cols],
                        term[:, cols],
                        ident[:],
                        start=(i == 0),
                        stop=(i == len(terms) - 1),
                        is_transpose=True,
                    )
            return bank

        def pair_tile(u):
            return keep.tile([P, 2, PAIR, HALF], F32, name=f"pairs{u}")

        lo, clamped, pairs, width = {}, {}, {}, {}
        quarters = [slice(0, QUARTER), slice(QUARTER, HALF)]
        last_pieces = [slice(0, QUARTER), slice(QUARTER, QUARTER + EIGHTH), slice(QUARTER + EIGHTH, HALF)]

        def fetch_pair(u):
            if u < AHEAD:
                pairs[u] = pair_tile(u)
            a, b = pairs[u][:, 0], pairs[u][:, 1]
            minus_b = unit_tile("minus_b")
            for t in range(PAIR):
                nc.vector.tensor_copy(b[:, t, :], looked_up(u, t, 1))
                nc.scalar.activation(minus_b[:, t, :], b[:, t, :], COPY, scale=-1.0)
                nc.vector.tensor_copy(a[:, t, :], looked_up(u, t, 0))
            diff = turned_sum([flat(minus_b[:]), flat(a)], "diff")
            width_turned = unit_tile(f"width_turned{u}")
            nc.scalar.activation(flat(width_turned[:]), diff[:], ABS)
            width[u] = turned_sum([flat(width_turned[:])], f"width{u % AHEAD}")

        def finish_unit(u):
            h, g = UNITS[u]
            last = u == len(UNITS) - 1
            a, b = pairs[u][:, 0], pairs[u][:, 1]
            lo[u] = clamped[u - 1] if u > 0 else unit_tile("lo0")
            clamped[u] = unit_tile(f"clamped{u}")
            pairs[u + AHEAD] = pair_tile(u + AHEAD)
            above = pairs[u + AHEAD][:].rearrange("p s t v -> p s (t v)")[:, :, QUARTER : QUARTER + HALF]
            result = median[h][:, PAIR * g : PAIR * (g + 1), :]
            bound = width[u][:].rearrange("p (t v) -> p t v", t=PAIR)
            for t in range(PAIR):
                nc.vector.tensor_tensor(lo[u][:, t, :], a[:, t, :], b[:, t, :], MIN)
            for t in range(PAIR):
                nc.vector.tensor_tensor(above[:, t, :], looked_up(u, t, 2), lo[u][:, t, :], SUB)
            if u + AHEAD < len(UNITS):
                for t in range(PAIR):
                    nc.vector.scalar_tensor_tensor(
                        clamped[u][:, t, :], above[:, t, :], 0.0, bound[:, t, :], MAX, MIN
                    )
                nc.gpsimd.tensor_tensor(flat(result), flat(clamped[u][:]), flat(lo[u][:]), ADD)
            else:
                for cols in quarters:
                    nc.vector.scalar_tensor_tensor(
                        clamped[u][:, :, cols], above[:, :, cols], 0.0, bound[:, :, cols], MAX, MIN
                    )
                for cols in last_pieces if last else quarters:
                    nc.vector.tensor_tensor(
                        result[:, :, cols], clamped[u][:, :, cols], lo[u][:, :, cols], ADD
                    )
            for cols in quarters if last else [slice(0, HALF)]:
                targets = slice(h * HALF + cols.start, h * HALF + cols.stop)
                nc.sync.dma_start(
                    out=out_rows[:, PAIR * g : PAIR * (g + 1), targets], in_=result[:, :, cols]
                )

        def store_codes(v0, n, calls, round_copy):
            h, c0 = divmod(v0, HALF)
            grouped = keep.tile([P, n, PACK], BF16, align_bytes=64, name=f"grouped{v0}")
            o_codes = keep.tile([P, n], U32, align_bytes=64, name=f"o_codes{v0}")
            starts = range(0, n, n // calls)
            for s in starts:
                round_copy(
                    out=grouped[:, s : s + n // calls, :].rearrange("p (c i) t -> p c t i", i=LINE),
                    in_=median[h][:, :, c0 + s : c0 + s + n // calls].rearrange("p t (c i) -> p c t i", i=LINE),
                )
            for s in starts:
                nc.vector.quantize_mx(
                    out=o_codes[:, s : s + n // calls].bitcast(FP8X4),
                    scales=o_plane[:, v0 + s : v0 + s + n // calls],
                    in_=grouped[:, s : s + n // calls, :].rearrange("p v t -> p (v t)"),
                )
            nc.sync.dma_start(
                out=out_words[:, PACK * v0 : PACK * (v0 + n)].bitcast(I32),
                in_=o_codes[:].bitcast(I32),
            )

        for u in range(AHEAD):
            fetch_pair(u)
        for u in range(len(UNITS) - 1):
            finish_unit(u)
            if u + AHEAD < len(UNITS):
                fetch_pair(u + AHEAD)
        store_codes(0, HALF, 1, nc.scalar.copy)
        finish_unit(len(UNITS) - 1)
        store_codes(HALF, QUARTER, 1, nc.scalar.copy)
        store_codes(HALF + QUARTER, QUARTER, 2, nc.vector.tensor_copy)

        for q in range(QUADRANTS):
            queue = nc.scalar if q % 2 == 0 else nc.sync
            queue.dma_start(
                out=out_2[0][4 * q : 4 * q + 4, :].bitcast(I32),
                in_=o_plane[32 * q : 32 * q + 4, :].bitcast(I32),
            )
